import numpy as np
import ml_dtypes


def mxq(x, axis, fmt="e4m3"):
    dtype, down = {"e4m3": (ml_dtypes.float8_e4m3fn, 7), "e5m2": (ml_dtypes.float8_e5m2, 14)}[fmt]
    v = np.moveaxis(np.asarray(x, np.float32).astype(ml_dtypes.bfloat16).astype(np.float64), axis, -1)
    blocks = v.reshape(v.shape[:-1] + (-1, 32))
    amax = np.abs(blocks).max(-1, keepdims=True)
    byte = np.maximum(np.where(amax > 0, np.frexp(amax)[1] - 1 + 127, 0) - down, 1)
    scale = np.exp2(byte - 127.0)
    codes = (blocks / scale).astype(np.float32).astype(dtype).astype(np.float64)
    return np.moveaxis((codes * scale).reshape(v.shape), -1, axis)


WIDE = False


def mx_kscale(k):
    if not WIDE:
        return np.ones(k)
    levels = np.array([10, -10, 5, -5, 0])
    if k % 512:
        return np.exp2(np.random.permutation(np.resize(levels, k // 32))).repeat(32)
    a = np.empty((k // 512, 16))
    for p in range(k // 512):
        a[p, :8] = np.random.permutation(np.resize(levels, 8))
        for g in range(8):
            far = levels[np.abs(levels - a[p, g]) >= 10]
            a[p, g + 8] = far[np.random.randint(len(far))]
    return np.exp2(a.ravel()).repeat(32)


def f64(x):
    return np.asarray(x).astype(np.float64)


def striped(idx):
    return np.tile(idx.reshape(-1, 16).T, (8, 1)).astype(np.uint16)


def unstriped(offs):
    return offs[:16].T.reshape(-1).astype(np.int64)


def striped8(idx):
    return np.concatenate([x.reshape(-1, 16).T for x in idx]).astype(np.uint16)


def runs(offs, k):
    lists = np.stack([offs[16 * r : 16 * r + 16].T.reshape(-1) for r in range(8)]).astype(np.int64)
    return lists[np.arange(k) % 512 // 64]


def pack_weight(w):
    k, n = w.shape
    w = f64(np.asarray(w, np.float32).astype(ml_dtypes.bfloat16)).reshape(k // 32, 32, n)
    amax = np.abs(w).max(1)
    byte = np.clip(np.where(amax > 0, np.frexp(amax)[1] - 1 + 127 - 7, 1), 1, 254)
    scaled = (w * np.exp2(127.0 - byte)[:, None, :]).reshape(k, n).astype(np.float32)
    words = np.ascontiguousarray(scaled.reshape(k // 512, 128, 4, n).transpose(0, 1, 3, 2)).astype(ml_dtypes.float8_e4m3fn).view(np.uint8)
    return words, np.ascontiguousarray(byte.astype(np.uint8).reshape(k // 512, 16, n))


def unpack_weight(words, scales):
    g, p, n, _ = words.shape
    vals = np.ascontiguousarray(words).view(ml_dtypes.float8_e4m3fn).astype(np.float64) * np.repeat(np.exp2(scales.astype(np.float64) - 127.0), 8, axis=1)[..., None]
    return vals.transpose(0, 1, 3, 2).reshape(g * 512, n)


E2M1 = np.array([0.0, 0.5, 1.0, 1.5, 2.0, 3.0, 4.0, 6.0, -0.0, -0.5, -1.0, -1.5, -2.0, -3.0, -4.0, -6.0])


def pack_fp4(w):
    k, n = w.shape
    w = f64(np.asarray(w, np.float32).astype(ml_dtypes.bfloat16)).reshape(k // 32, 32, n)
    amax = np.abs(w).max(1)
    mant, ex = np.frexp(amax / 6.0)
    byte = np.clip(np.where(amax > 0, np.where(mant > 0.5, ex, ex - 1) + 127, 1), 1, 254)
    scaled = (w * np.exp2(127.0 - byte)[:, None, :]).reshape(k, n).astype(np.float32)
    c = np.ascontiguousarray(scaled.reshape(k // 512, 128, 4, n).transpose(0, 1, 3, 2)).astype(ml_dtypes.float4_e2m1fn).view(np.uint8) & 0xF
    words = (c[..., 0::2] | (c[..., 1::2] << 4)).reshape(k // 512, 128, 2 * n)
    return np.ascontiguousarray(words), np.ascontiguousarray(byte.astype(np.uint8).reshape(k // 512, 16, n))


def unpack_fp4(words, scales):
    g, _, n = scales.shape
    words = np.ascontiguousarray(words).reshape(g, 128, n, 2)
    nib = np.empty((g, 128, n, 4), np.uint8)
    nib[..., 0::2] = words & 0xF
    nib[..., 1::2] = words >> 4
    vals = E2M1[nib] * np.repeat(np.exp2(scales.astype(np.float64) - 127.0), 8, axis=1)[..., None]
    return vals.transpose(0, 1, 3, 2).reshape(g * 512, n)


def sigmoid(v):
    return 1.0 / (1.0 + np.exp(-np.maximum(v, -700.0)))

def planes(y):
    n, m = y.shape
    v = y.astype(np.float32).astype(ml_dtypes.bfloat16).astype(np.float64).reshape(n // 32, 32, m)
    top = np.abs(v).max(1)
    byte = np.clip(np.where(top > 0, np.frexp(top)[1] - 1 + 127 - 7, 1), 1, 254)
    codes = (v * np.exp2(127.0 - byte)[:, None, :]).reshape(n, m).astype(np.float32).astype(ml_dtypes.float8_e4m3fn).view(np.uint8)
    words = codes.reshape(n // 512, 128, 4, m).transpose(0, 1, 3, 2)
    return np.ascontiguousarray(words), np.ascontiguousarray(byte.astype(np.uint8).reshape(n // 512, 16, m))


K, T, S, N, H = 512, 2048, 512, 512, 512


def setup_inputs():
    n = np.random.standard_normal
    s = mx_kscale(K)[:, None]
    u = mx_kscale(H)
    packed_xT = pack_weight(n((K, T)) * s)
    packed_w1 = pack_fp4(n((K, H)) / np.sqrt(K) / s)
    packed_w2 = pack_fp4(n((H, N)) / np.sqrt(H) / u[:, None])
    return {
        "x_words": packed_xT[0],
        "x_scales": packed_xT[1],
        "w1_words": packed_w1[0],
        "w1_scales": packed_w1[1],
        "gn": (np.random.uniform(0.5, 1.5, (H, 1)) * u[:, None]).astype(np.float32),
        "w2_words": packed_w2[0],
        "w2_scales": packed_w2[1],
        "offs": striped(np.random.permutation(T)[:S]),
        "n1": striped8(np.stack([np.random.permutation(S) for _ in range(8)])),
        "n2": striped8(np.stack([np.random.permutation(S) for _ in range(8)])),
        "n3": striped8(np.stack([np.random.permutation(S) for _ in range(8)])),
    }


def reference(x_words, x_scales, w1_words, w1_scales, gn, w2_words, w2_scales, offs, n1, n2, n3):
    xq = unpack_weight(x_words, x_scales)[:, unstriped(offs)]
    y = unpack_fp4(w1_words, w1_scales).T @ xq
    st = y * (sigmoid(y[np.arange(H)[:, None], runs(n1, H)]))
    z = f64(gn) * (np.maximum(st, st[np.arange(H)[:, None], runs(n1, H)]))
    h = unpack_fp4(w2_words, w2_scales).T @ mxq(z, 0, "e4m3")
    out_0 = 0.75 * (h * (y[np.arange(H)[:, None], runs(n3, H)]) - ((h[np.arange(N)[:, None], runs(n2, N)]) * y))
    return (out_0,) + planes(out_0)

@@ -1,0 +1,180 @@
+from contextlib import ExitStack
+
+import concourse.mybir as mybir
+
+K, T, S, H, N = 512, 2048, 512, 512, 512
+FLOPS = 2 * K * H * S + 2 * H * N * S
+
+F32 = mybir.dt.float32
+BF16 = mybir.dt.bfloat16
+I32 = mybir.dt.int32
+U32 = mybir.dt.uint32
+U16 = mybir.dt.uint16
+U8 = mybir.dt.uint8
+FP8X4 = mybir.dt.float8_e4m3fn_x4
+FP4X4 = mybir.dt.float4_e2m1fn_x4
+ALU = mybir.AluOpType
+ACT = mybir.ActivationFunctionType
+
+P = 128
+PACK = 4
+HALF = S // 2
+HALVES = [slice(0, HALF), slice(HALF, S)]
+
+
+def entries(lst, cols):
+    return lst[:, cols.start // 16 : cols.stop // 16]
+
+
+def load_scale_rows(nc, plane, rows):
+    for q in range(4):
+        nc.sync.dma_start(out=plane[32 * q : 32 * q + 4, :].bitcast(I32), in_=rows[4 * q : 4 * q + 4, :].bitcast(I32))
+
+
+def tile_picked_skipcrossbtwicp_none_po_kernel(
+    tc, x_words, x_scales, w1_words, w1_scales, gn, w2_words, w2_scales, offs, n1, n2, n3, out_0, out_1, out_2
+):
+    nc = tc.nc
+    with ExitStack() as ctx:
+        sb = ctx.enter_context(tc.tile_pool(name="sb", bufs=1))
+        ps = ctx.enter_context(tc.psum_pool(name="ps", bufs=1))
+
+        def tile(name, shape, dtype):
+            return sb.tile(shape, dtype, name=name, align_bytes=64)
+
+        def bank(b):
+            return ps.tile([P, 512], F32, name="bank%d" % b)
+
+        offs_sb = tile("offs_sb", [P, S // 16], U16)
+        n1_sb = tile("n1_sb", [P, S // 16], U16)
+        n2_sb = tile("n2_sb", [P, S // 16], U16)
+        n3_sb = tile("n3_sb", [P, S // 16], U16)
+        xw = tile("xw", [P, T], I32)
+        xs = tile("xs", [P, T], U8)
+        w1w = tile("w1w", [P, 2 * H], U8)
+        w1s = tile("w1s", [P, H], U8)
+        w2w = tile("w2w", [P, 2 * N], U8)
+        w2s = tile("w2s", [P, N], U8)
+        gain = tile("gain", [P, PACK], F32)
+
+        nc.vector.memset(xs[:].bitcast(I32), 0)
+        nc.gpsimd.memset(w1s[:].bitcast(I32), 0)
+        nc.gpsimd.memset(w2s[:].bitcast(I32), 0)
+        nc.sync.dma_start(offs_sb[:], offs)
+        load_scale_rows(nc, xs, x_scales[0])
+        nc.sync.dma_start(out=w1w[:].bitcast(I32), in_=w1_words[0].bitcast(I32))
+        nc.sync.dma_start(out=xw[:], in_=x_words[0].rearrange("p n t -> p (n t)").bitcast(I32))
+        load_scale_rows(nc, w1s, w1_scales[0])
+        nc.sync.dma_start(n1_sb[:], n1)
+        nc.sync.dma_start(out=gain[:], in_=gn.rearrange("(p t) o -> p (t o)", t=PACK))
+        nc.sync.dma_start(out=w2w[:].bitcast(I32), in_=w2_words[0].bitcast(I32))
+        load_scale_rows(nc, w2s, w2_scales[0])
+        nc.sync.dma_start(n3_sb[:], n3)
+        nc.sync.dma_start(n2_sb[:], n2)
+
+        def deal(name, words, scales):
+            dw = tile(name + "_dw", [P, PACK, P, 2], U8)
+            ds = tile(name + "_ds", [P, PACK, P], U8)
+            nc.vector.tensor_copy(out=dw[:], in_=words[:].rearrange("p (m t b) -> p t m b", t=PACK, b=2))
+            nc.vector.tensor_copy(out=ds[:], in_=scales[:].rearrange("p (m t) -> p t m", t=PACK))
+            return dw, ds
+
+        def product(acc, dealt, t, codes, scales):
+            dw, ds = dealt
+            nc.tensor.matmul_mx(
+                out=acc,
+                lhsT=dw[:, t, :, :].rearrange("p m b -> p (m b)").bitcast(FP4X4),
+                lhsT_scale=ds[:, t, :],
+                rhs=codes.bitcast(FP8X4),
+                rhs_scale=scales,
+                start=True,
+                stop=True,
+            )
+
+        xgs = tile("xgs", [P, S], U8)
+        xgw = tile("xgw", [P, S], U32)
+        nc.vector.tensor_copy(out=xgs[:], in_=xs[:].indirect(offs_sb[:]))
+        w1d = deal("w1", w1w, w1s)
+        for cols in HALVES:
+            nc.vector.tensor_copy(out=xgw[:, cols], in_=xw[:].bitcast(U32).indirect(entries(offs_sb, cols)))
+
+        y = [tile("y%d" % t, [P, S], F32) for t in range(PACK)]
+        pieces = [(0, HALVES[0]), (1, HALVES[0]), (0, HALVES[1]), (1, HALVES[1]), (2, slice(0, S)), (3, slice(0, S))]
+        accs = []
+        for b, (t, cols) in enumerate(pieces):
+            acc = bank(b)
+            width = cols.stop - cols.start
+            product(acc[:, 0:width], w1d, t, xgw[:, cols], xgs[:, cols])
+            accs.append(acc[:, 0:width])
+        for acc, (t, cols) in zip(accs, pieces):
+            if t == 0:
+                nc.scalar.copy(out=y[t][:, cols], in_=acc)
+            else:
+                nc.vector.tensor_copy(out=y[t][:, cols], in_=acc)
+
+        sg = [tile("sg%d" % t, [P, S], F32) for t in range(PACK)]
+        st = [tile("st%d" % t, [P, S], F32) for t in range(PACK)]
+        stg = [tile("stg%d" % h, [P, PACK, HALF], F32) for h in range(2)]
+        mx = [tile("mx%d" % h, [P, PACK, HALF], F32) for h in range(2)]
+        zp = [tile("zp%d" % h, [P, PACK, HALF], BF16) for h in range(2)]
+        zi = [tile("zi%d" % h, [P, HALF, PACK], BF16) for h in range(2)]
+        zw = tile("zw", [P, S], U32)
+        zs = tile("zs", [P, S], U8)
+
+        for t in range(PACK):
+            for cols in HALVES:
+                nc.scalar.activation(out=sg[t][:, cols], in_=y[t][:].indirect(entries(n1_sb, cols)), func=ACT.Sigmoid)
+
+        def larger(t, h):
+            cols = HALVES[h]
+            nc.vector.tensor_copy(out=stg[h][:, t, :], in_=st[t][:].indirect(entries(n1_sb, cols)))
+            nc.vector.tensor_tensor(out=mx[h][:, t, :], in0=stg[h][:, t, :], in1=st[t][:, cols], op=ALU.max)
+            nc.scalar.activation(out=zp[h][:, t, :], in_=mx[h][:, t, :], func=ACT.Copy, scale=gain[:, t : t + 1])
+
+        def weave(engine_copy, dst, src):
+            engine_copy(
+                out=dst.rearrange("p (c i) t -> p c t i", i=2),
+                in_=src.rearrange("p t (c i) -> p c t i", i=2),
+            )
+
+        hh = [tile("h%d" % t, [P, S], F32) for t in range(PACK)]
+
+        def second(h, w2d):
+            cols = HALVES[h]
+            weave(nc.scalar.copy, zi[h][:], zp[h][:])
+            nc.vector.quantize_mx(out=zw[:, cols].bitcast(FP8X4), scales=zs[:, cols], in_=zi[h][:].rearrange("p c t -> p (c t)"))
+            for t in range(PACK):
+                acc = bank(PACK * h + t)
+                product(acc[:, 0:HALF], w2d, t, zw[:, cols], zs[:, cols])
+                nc.scalar.activation(out=hh[t][:, cols], in_=acc[:, 0:HALF], func=ACT.Copy, scale=0.75)
+
+        for t in range(PACK):
+            nc.vector.tensor_tensor(out=st[t][:], in0=y[t][:], in1=sg[t][:], op=ALU.mult)
+            larger(t, 0)
+        w2d = deal("w2", w2w, w2s)
+        second(0, w2d)
+        for t in range(PACK):
+            larger(t, 1)
+        second(1, w2d)
+
+        ow = tile("ow", [P, S], I32)
+        osc = tile("osc", [P, S], U8)
+        out_rows = out_0.rearrange("(p t) j -> p t j", t=PACK)
+        out_words = out_1[0].rearrange("p n t -> p (n t)").bitcast(I32)
+        for h, cols in enumerate(HALVES):
+            p1 = tile("p1_%d" % h, [P, PACK, HALF], F32)
+            p2 = tile("p2_%d" % h, [P, PACK, HALF], F32)
+            res = tile("res%d" % h, [P, PACK, HALF], F32)
+            ri = tile("ri%d" % h, [P, HALF, PACK], BF16)
+            for t in range(PACK):
+                nc.vector.tensor_tensor(out=p1[:, t, :], in0=y[t][:].indirect(entries(n3_sb, cols)), in1=hh[t][:, cols], op=ALU.mult)
+            for t in range(PACK):
+                nc.vector.tensor_tensor(out=p2[:, t, :], in0=hh[t][:].indirect(entries(n2_sb, cols)), in1=y[t][:, cols], op=ALU.mult)
+            nc.vector.tensor_tensor(out=res[:], in0=p1[:], in1=p2[:], op=ALU.subtract)
+            nc.sync.dma_start(out=out_rows[:, :, cols], in_=res[:])
+            weave(nc.scalar.copy if h == 0 else nc.vector.tensor_copy, ri[:], res[:])
+            nc.vector.quantize_mx(out=ow[:, cols].bitcast(FP8X4), scales=osc[:, cols], in_=ri[:].rearrange("p c t -> p (c t)"))
+            nc.sync.dma_start(out=out_words[:, cols], in_=ow[:, cols])
+        for q in range(4):
+            queue = nc.scalar if q % 2 else nc.sync
+            queue.dma_start(out=out_2[0][4 * q : 4 * q + 4, :].bitcast(I32), in_=osc[32 * q : 32 * q + 4, :].bitcast(I32))

@@ -19,6 +19,7 @@ ACT = mybir.ActivationFunctionType
 P = 128
 PACK = 4
 HALF = S // 2
+ALL = slice(0, S)
 HALVES = [slice(0, HALF), slice(HALF, S)]
 
 
@@ -26,9 +27,9 @@ def entries(lst, cols):
     return lst[:, cols.start // 16 : cols.stop // 16]
 
 
-def load_scale_rows(nc, plane, rows):
+def load_scale_rows(queues, plane, rows):
     for q in range(4):
-        nc.sync.dma_start(out=plane[32 * q : 32 * q + 4, :].bitcast(I32), in_=rows[4 * q : 4 * q + 4, :].bitcast(I32))
+        queues[q].dma_start(out=plane[32 * q : 32 * q + 4, :].bitcast(I32), in_=rows[4 * q : 4 * q + 4, :].bitcast(I32))
 
 
 def tile_picked_skipcrossbtwicp_none_po_kernel(
@@ -39,8 +40,8 @@ def tile_picked_skipcrossbtwicp_none_po_kernel(
         sb = ctx.enter_context(tc.tile_pool(name="sb", bufs=1))
         ps = ctx.enter_context(tc.psum_pool(name="ps", bufs=1))
 
-        def tile(name, shape, dtype):
-            return sb.tile(shape, dtype, name=name, align_bytes=64)
+        def tile(name, shape, dtype, tag=None):
+            return sb.tile(shape, dtype, name=name, tag=tag or name, align_bytes=64)
 
         def bank(b):
             return ps.tile([P, 512], F32, name="bank%d" % b)
@@ -51,36 +52,31 @@ def tile_picked_skipcrossbtwicp_none_po_kernel(
         n3_sb = tile("n3_sb", [P, S // 16], U16)
         xw = tile("xw", [P, T], I32)
         xs = tile("xs", [P, T], U8)
-        w1w = tile("w1w", [P, 2 * H], U8)
-        w1s = tile("w1s", [P, H], U8)
-        w2w = tile("w2w", [P, 2 * N], U8)
-        w2s = tile("w2s", [P, N], U8)
-        gain = tile("gain", [P, PACK], F32)
+        ww = tile("ww", [P, 2 * H], U8)
+        ws = tile("ws", [P, H], U8)
 
+        nc.gpsimd.memset(ws[:].bitcast(I32), 0)
         nc.vector.memset(xs[:].bitcast(I32), 0)
-        nc.gpsimd.memset(w1s[:].bitcast(I32), 0)
-        nc.gpsimd.memset(w2s[:].bitcast(I32), 0)
         nc.sync.dma_start(offs_sb[:], offs)
-        load_scale_rows(nc, xs, x_scales[0])
-        nc.sync.dma_start(out=w1w[:].bitcast(I32), in_=w1_words[0].bitcast(I32))
-        nc.sync.dma_start(out=xw[:], in_=x_words[0].rearrange("p n t -> p (n t)").bitcast(I32))
-        load_scale_rows(nc, w1s, w1_scales[0])
+        nc.sync.dma_start(out=ww[:].bitcast(I32), in_=w1_words[0].bitcast(I32))
         nc.sync.dma_start(n1_sb[:], n1)
-        nc.sync.dma_start(out=gain[:], in_=gn.rearrange("(p t) o -> p (t o)", t=PACK))
-        nc.sync.dma_start(out=w2w[:].bitcast(I32), in_=w2_words[0].bitcast(I32))
-        load_scale_rows(nc, w2s, w2_scales[0])
         nc.sync.dma_start(n3_sb[:], n3)
         nc.sync.dma_start(n2_sb[:], n2)
+        nc.sync.dma_start(out=xw[:], in_=x_words[0].rearrange("p n t -> p (n t)").bitcast(I32))
+        load_scale_rows([nc.scalar] * 4, xs, x_scales[0])
+        load_scale_rows([nc.gpsimd] + [nc.scalar] * 3, ws, w1_scales[0])
 
-        def deal(name, words, scales):
-            dw = tile(name + "_dw", [P, PACK, P, 2], U8)
-            ds = tile(name + "_ds", [P, PACK, P], U8)
+        def deal_words(name, words):
+            dw = tile(name, [P, PACK, P, 2], U8)
             nc.vector.tensor_copy(out=dw[:], in_=words[:].rearrange("p (m t b) -> p t m b", t=PACK, b=2))
-            nc.vector.tensor_copy(out=ds[:], in_=scales[:].rearrange("p (m t) -> p t m", t=PACK))
-            return dw, ds
+            return dw
 
-        def product(acc, dealt, t, codes, scales):
-            dw, ds = dealt
+        def deal_scales(name, scales):
+            ds = tile(name, [P, PACK, P], U8)
+            nc.vector.tensor_copy(out=ds[:], in_=scales[:].rearrange("p (m t) -> p t m", t=PACK))
+            return ds
+
+        def product(acc, dw, ds, t, codes, scales):
             nc.tensor.matmul_mx(
                 out=acc,
                 lhsT=dw[:, t, :, :].rearrange("p m b -> p (m b)").bitcast(FP4X4),
@@ -91,90 +87,155 @@ def tile_picked_skipcrossbtwicp_none_po_kernel(
                 stop=True,
             )
 
-        xgs = tile("xgs", [P, S], U8)
-        xgw = tile("xgw", [P, S], U32)
-        nc.vector.tensor_copy(out=xgs[:], in_=xs[:].indirect(offs_sb[:]))
-        w1d = deal("w1", w1w, w1s)
-        for cols in HALVES:
-            nc.vector.tensor_copy(out=xgw[:, cols], in_=xw[:].bitcast(U32).indirect(entries(offs_sb, cols)))
-
-        y = [tile("y%d" % t, [P, S], F32) for t in range(PACK)]
-        pieces = [(0, HALVES[0]), (1, HALVES[0]), (0, HALVES[1]), (1, HALVES[1]), (2, slice(0, S)), (3, slice(0, S))]
-        accs = []
-        for b, (t, cols) in enumerate(pieces):
-            acc = bank(b)
-            width = cols.stop - cols.start
-            product(acc[:, 0:width], w1d, t, xgw[:, cols], xgs[:, cols])
-            accs.append(acc[:, 0:width])
-        for acc, (t, cols) in zip(accs, pieces):
-            if t == 0:
-                nc.scalar.copy(out=y[t][:, cols], in_=acc)
-            else:
-                nc.vector.tensor_copy(out=y[t][:, cols], in_=acc)
-
-        sg = [tile("sg%d" % t, [P, S], F32) for t in range(PACK)]
-        st = [tile("st%d" % t, [P, S], F32) for t in range(PACK)]
-        stg = [tile("stg%d" % h, [P, PACK, HALF], F32) for h in range(2)]
-        mx = [tile("mx%d" % h, [P, PACK, HALF], F32) for h in range(2)]
-        zp = [tile("zp%d" % h, [P, PACK, HALF], BF16) for h in range(2)]
-        zi = [tile("zi%d" % h, [P, HALF, PACK], BF16) for h in range(2)]
-        zw = tile("zw", [P, S], U32)
-        zs = tile("zs", [P, S], U8)
-
-        for t in range(PACK):
-            for cols in HALVES:
-                nc.scalar.activation(out=sg[t][:, cols], in_=y[t][:].indirect(entries(n1_sb, cols)), func=ACT.Sigmoid)
-
-        def larger(t, h):
-            cols = HALVES[h]
-            nc.vector.tensor_copy(out=stg[h][:, t, :], in_=st[t][:].indirect(entries(n1_sb, cols)))
-            nc.vector.tensor_tensor(out=mx[h][:, t, :], in0=stg[h][:, t, :], in1=st[t][:, cols], op=ALU.max)
-            nc.scalar.activation(out=zp[h][:, t, :], in_=mx[h][:, t, :], func=ACT.Copy, scale=gain[:, t : t + 1])
-
         def weave(engine_copy, dst, src):
             engine_copy(
                 out=dst.rearrange("p (c i) t -> p c t i", i=2),
                 in_=src.rearrange("p t (c i) -> p c t i", i=2),
             )
 
-        hh = [tile("h%d" % t, [P, S], F32) for t in range(PACK)]
+        w1dw = deal_words("w1dw", ww)
+        gain = tile("gain", [P, PACK], F32, tag="ww")
+        nc.sync.dma_start(out=gain[:], in_=gn.rearrange("(p t) o -> p (t o)", t=PACK))
+        w1ds = deal_scales("w1ds", ws)
+        load_scale_rows([nc.sync] * 4, ws, w2_scales[0])
+        xgs = [tile("xgs%d" % h, [P, HALF], U8) for h in range(2)]
+        xgw = [tile("xgw%d" % h, [P, HALF], U32) for h in range(2)]
+        for h, cols in enumerate(HALVES):
+            nc.vector.tensor_copy(out=xgs[h][:], in_=xs[:].indirect(entries(offs_sb, cols)))
+            nc.vector.tensor_copy(out=xgw[h][:], in_=xw[:].bitcast(U32).indirect(entries(offs_sb, cols)))
+        ww2 = tile("ww2", [P, 2 * N], U8, tag="xs")
+        nc.sync.dma_start(out=ww2[:].bitcast(I32), in_=w2_words[0].bitcast(I32))
 
-        def second(h, w2d):
+        y = [tile("y%d" % t, [P, S], F32) for t in range(PACK)]
+        accs = {}
+        for t, h in [(0, 0), (1, 0), (0, 1), (1, 1)]:
+            accs[t, h] = bank(2 * t + h)[:, 0:HALF]
+            product(accs[t, h], w1dw, w1ds, t, xgw[h][:], xgs[h][:])
+        for t in (2, 3):
+            accs[t] = bank(2 + t)
+            for h, cols in enumerate(HALVES):
+                product(accs[t][:, cols], w1dw, w1ds, t, xgw[h][:], xgs[h][:])
+
+        sg0 = tile("sg0", [P, S], F32)
+        stw = [tile("stw%d" % t, [P, S], F32) for t in range(PACK)]
+        sg = [None] + [tile("sg%d" % t, [P, S], F32) for t in range(1, PACK)]
+        hw = [tile("hw%d" % t, [P, 2 * S], F32) for t in range(PACK)]
+        st = [w[:, 0:S] for w in stw]
+        hh = [w[:, 0:S] for w in hw]
+        stg = [w[:, S : 2 * S] for w in hw]
+        mx = tile("mx", [P, PACK, S], F32)
+        zp = [tile("zp%d" % h, [P, PACK, HALF], BF16) for h in range(2)]
+        zi = [tile("zi%d" % h, [P, HALF, PACK], BF16) for h in range(2)]
+        zw = [tile("zw%d" % h, [P, HALF], U32) for h in range(2)]
+        zs = [tile("zs%d" % h, [P, HALF], U8) for h in range(2)]
+
+        def gather_st(t, h):
             cols = HALVES[h]
-            weave(nc.scalar.copy, zi[h][:], zp[h][:])
-            nc.vector.quantize_mx(out=zw[:, cols].bitcast(FP8X4), scales=zs[:, cols], in_=zi[h][:].rearrange("p c t -> p (c t)"))
+            nc.vector.tensor_copy(out=stg[t][:, cols], in_=stw[t][:].indirect(entries(n1_sb, cols)))
+
+        def larger(t, h):
+            cols = HALVES[h]
+            nc.vector.tensor_tensor(out=mx[:, t, cols], in0=stg[t][:, cols], in1=st[t][:, cols], op=ALU.max)
+            nc.scalar.activation(out=zp[h][:, t, :], in_=mx[:, t, cols], func=ACT.Copy, scale=gain[:, t : t + 1])
+
+        def gate(t):
+            for cols in HALVES:
+                nc.scalar.activation(out=sg[t][:, cols], in_=y[t][:].indirect(entries(n1_sb, cols)), func=ACT.Sigmoid)
+
+        def gated(t):
+            nc.vector.tensor_tensor(out=st[t], in0=y[t][:], in1=sg[t][:], op=ALU.mult)
+
+        def quantize_z(h):
+            nc.vector.quantize_mx(out=zw[h][:].bitcast(FP8X4), scales=zs[h][:], in_=zi[h][:].rearrange("p c t -> p (c t)"))
+
+        def second(h):
             for t in range(PACK):
-                acc = bank(PACK * h + t)
-                product(acc[:, 0:HALF], w2d, t, zw[:, cols], zs[:, cols])
-                nc.scalar.activation(out=hh[t][:, cols], in_=acc[:, 0:HALF], func=ACT.Copy, scale=0.75)
+                acc = bank(PACK * h + t)[:, 0:HALF]
+                product(acc, w2dw, w2ds, t, zw[h][:], zs[h][:])
+                nc.scalar.activation(out=hh[t][:, HALVES[h]], in_=acc, func=ACT.Copy, scale=0.75)
 
-        for t in range(PACK):
-            nc.vector.tensor_tensor(out=st[t][:], in0=y[t][:], in1=sg[t][:], op=ALU.mult)
-            larger(t, 0)
-        w2d = deal("w2", w2w, w2s)
-        second(0, w2d)
-        for t in range(PACK):
-            larger(t, 1)
-        second(1, w2d)
+        for h, cols in enumerate(HALVES):
+            nc.scalar.activation(out=sg0[:, cols], in_=accs[0, h], func=ACT.Sigmoid)
+            nc.vector.tensor_copy(out=y[0][:, cols], in_=accs[0, h])
+            nc.scalar.copy(out=y[1][:, cols], in_=accs[1, h])
+        gate(1)
+        for t in (2, 3):
+            nc.scalar.copy(out=y[t][:], in_=accs[t][:])
+            gate(t)
+        for cols in HALVES:
+            nc.vector.tensor_tensor(out=st[0][:, cols], in0=sg0[:].indirect(entries(n1_sb, cols)), in1=y[0][:, cols], op=ALU.mult)
+        w2dw = deal_words("w2dw", ww2)
+        gather_st(0, 0)
+        gated(1)
+        larger(0, 0)
+        gather_st(1, 0)
+        gather_st(0, 1)
+        gated(2)
+        larger(1, 0)
+        gather_st(2, 0)
+        gated(3)
+        larger(2, 0)
+        gather_st(3, 0)
+        larger(0, 1)
+        larger(3, 0)
+        weave(nc.scalar.copy, zi[0][:], zp[0][:])
+        w2ds = deal_scales("w2ds", ws)
+        gather_st(1, 1)
+        gather_st(2, 1)
+        larger(1, 1)
+        gather_st(3, 1)
+        larger(2, 1)
+        quantize_z(0)
+        larger(3, 1)
+        second(0)
 
+        p1 = tile("p1", [P, PACK, S], F32)
+        p2 = tile("p2", [P, PACK, S], F32)
+        res = tile("res", [P, PACK, S], F32)
+        ri = [tile("ri%d" % h, [P, HALF, PACK], BF16) for h in range(2)]
         ow = tile("ow", [P, S], I32)
         osc = tile("osc", [P, S], U8)
         out_rows = out_0.rearrange("(p t) j -> p t j", t=PACK)
         out_words = out_1[0].rearrange("p n t -> p (n t)").bitcast(I32)
-        for h, cols in enumerate(HALVES):
-            p1 = tile("p1_%d" % h, [P, PACK, HALF], F32)
-            p2 = tile("p2_%d" % h, [P, PACK, HALF], F32)
-            res = tile("res%d" % h, [P, PACK, HALF], F32)
-            ri = tile("ri%d" % h, [P, HALF, PACK], BF16)
-            for t in range(PACK):
-                nc.vector.tensor_tensor(out=p1[:, t, :], in0=y[t][:].indirect(entries(n3_sb, cols)), in1=hh[t][:, cols], op=ALU.mult)
-            for t in range(PACK):
-                nc.vector.tensor_tensor(out=p2[:, t, :], in0=hh[t][:].indirect(entries(n2_sb, cols)), in1=y[t][:, cols], op=ALU.mult)
-            nc.vector.tensor_tensor(out=res[:], in0=p1[:], in1=p2[:], op=ALU.subtract)
-            nc.sync.dma_start(out=out_rows[:, :, cols], in_=res[:])
-            weave(nc.scalar.copy if h == 0 else nc.vector.tensor_copy, ri[:], res[:])
-            nc.vector.quantize_mx(out=ow[:, cols].bitcast(FP8X4), scales=osc[:, cols], in_=ri[:].rearrange("p c t -> p (c t)"))
+
+        def first_term(t, cols):
+            nc.vector.tensor_tensor(out=p1[:, t, cols], in0=y[t][:].indirect(entries(n3_sb, cols)), in1=hh[t][:, cols], op=ALU.mult)
+
+        def second_term(t, cols):
+            nc.vector.tensor_tensor(out=p2[:, t, cols], in0=hw[t][:].indirect(entries(n2_sb, cols)), in1=y[t][:, cols], op=ALU.mult)
+
+        def difference(t, cols):
+            nc.vector.tensor_tensor(out=res[:, t, cols], in0=p1[:, t, cols], in1=p2[:, t, cols], op=ALU.subtract)
+            nc.sync.dma_start(out=out_rows[:, t, cols], in_=res[:, t, cols])
+
+        def planes(h):
+            cols = HALVES[h]
+            nc.vector.quantize_mx(out=ow[:, cols].bitcast(FP8X4), scales=osc[:, cols], in_=ri[h][:].rearrange("p c t -> p (c t)"))
             nc.sync.dma_start(out=out_words[:, cols], in_=ow[:, cols])
+
+        first_term(0, HALVES[0])
+        weave(nc.vector.tensor_copy, zi[1][:], zp[1][:])
+        first_term(1, HALVES[0])
+        quantize_z(1)
+        second(1)
+        first_term(2, HALVES[0])
+        first_term(3, HALVES[0])
+        for t in range(PACK - 1):
+            second_term(t, ALL)
+            first_term(t, HALVES[1])
+            if t > 0:
+                difference(t - 1, ALL)
+        last = PACK - 1
+        second_term(last, HALVES[0])
+        difference(last - 1, ALL)
+        difference(last, HALVES[0])
+        weave(nc.scalar.copy, ri[0][:], res[:, :, HALVES[0]])
+        first_term(last, HALVES[1])
+        second_term(last, HALVES[1])
+        difference(last, HALVES[1])
+        planes(0)
+        weave(nc.vector.tensor_copy, ri[1][:], res[:, :, HALVES[1]])
+        planes(1)
         for q in range(4):
             queue = nc.scalar if q % 2 else nc.sync
             queue.dma_start(out=out_2[0][4 * q : 4 * q + 4, :].bitcast(I32), in_=osc[32 * q : 32 * q + 4, :].bitcast(I32))

@@ -1,6 +1,7 @@
 from contextlib import ExitStack
 
 import concourse.mybir as mybir
+from concourse.masks import make_identity
 
 K, T, S, H, N = 512, 2048, 512, 512, 512
 FLOPS = 2 * K * H * S + 2 * H * N * S
@@ -21,6 +22,8 @@ PACK = 4
 HALF = S // 2
 ALL = slice(0, S)
 HALVES = [slice(0, HALF), slice(HALF, S)]
+SUMMED = [(0, 0), (0, 1), (1, 0)]
+QUARTERS = [slice(256, 384), slice(384, 512)]
 
 
 def entries(lst, cols):
@@ -55,13 +58,15 @@ def tile_picked_skipcrossbtwicp_none_po_kernel(
         ww = tile("ww", [P, 2 * H], U8)
         ws = tile("ws", [P, H], U8)
 
+        nc.gpsimd.memset(xs[:].bitcast(I32), 0)
         nc.gpsimd.memset(ws[:].bitcast(I32), 0)
-        nc.vector.memset(xs[:].bitcast(I32), 0)
         nc.sync.dma_start(offs_sb[:], offs)
         nc.sync.dma_start(out=ww[:].bitcast(I32), in_=w1_words[0].bitcast(I32))
         nc.sync.dma_start(n1_sb[:], n1)
         nc.sync.dma_start(n3_sb[:], n3)
         nc.sync.dma_start(n2_sb[:], n2)
+        ww2 = tile("ww2", [P, 2 * N], U8)
+        nc.sync.dma_start(out=ww2[:].bitcast(I32), in_=w2_words[0].bitcast(I32))
         nc.sync.dma_start(out=xw[:], in_=x_words[0].rearrange("p n t -> p (n t)").bitcast(I32))
         load_scale_rows([nc.scalar] * 4, xs, x_scales[0])
         load_scale_rows([nc.gpsimd] + [nc.scalar] * 3, ws, w1_scales[0])
@@ -96,6 +101,7 @@ def tile_picked_skipcrossbtwicp_none_po_kernel(
         w1dw = deal_words("w1dw", ww)
         gain = tile("gain", [P, PACK], F32, tag="ww")
         nc.sync.dma_start(out=gain[:], in_=gn.rearrange("(p t) o -> p (t o)", t=PACK))
+        w2dw = deal_words("w2dw", ww2)
         w1ds = deal_scales("w1ds", ws)
         load_scale_rows([nc.sync] * 4, ws, w2_scales[0])
         xgs = [tile("xgs%d" % h, [P, HALF], U8) for h in range(2)]
@@ -103,8 +109,6 @@ def tile_picked_skipcrossbtwicp_none_po_kernel(
         for h, cols in enumerate(HALVES):
             nc.vector.tensor_copy(out=xgs[h][:], in_=xs[:].indirect(entries(offs_sb, cols)))
             nc.vector.tensor_copy(out=xgw[h][:], in_=xw[:].bitcast(U32).indirect(entries(offs_sb, cols)))
-        ww2 = tile("ww2", [P, 2 * N], U8, tag="xs")
-        nc.sync.dma_start(out=ww2[:].bitcast(I32), in_=w2_words[0].bitcast(I32))
 
         y = [tile("y%d" % t, [P, S], F32) for t in range(PACK)]
         accs = {}
@@ -124,6 +128,9 @@ def tile_picked_skipcrossbtwicp_none_po_kernel(
         hh = [w[:, 0:S] for w in hw]
         stg = [w[:, S : 2 * S] for w in hw]
         mx = tile("mx", [P, PACK, S], F32)
+        hp = {(t, h): tile("hp%d%d" % (t, h), [P, HALF], F32) for t, h in SUMMED}
+        ident = tile("ident", [P, P], F32)
+        make_identity(nc, ident[:])
         zp = [tile("zp%d" % h, [P, PACK, HALF], BF16) for h in range(2)]
         zi = [tile("zi%d" % h, [P, HALF, PACK], BF16) for h in range(2)]
         zw = [tile("zw%d" % h, [P, HALF], U32) for h in range(2)]
@@ -152,19 +159,37 @@ def tile_picked_skipcrossbtwicp_none_po_kernel(
             for t in range(PACK):
                 acc = bank(PACK * h + t)[:, 0:HALF]
                 product(acc, w2dw, w2ds, t, zw[h][:], zs[h][:])
-                nc.scalar.activation(out=hh[t][:, HALVES[h]], in_=acc, func=ACT.Copy, scale=0.75)
+                copies = [(hh[t][:, HALVES[h]], -0.75)] + ([(hp[t, h][:], 0.75)] if (t, h) in SUMMED else [])
+                for dst, factor in copies[::-1] if h == 0 else copies:
+                    nc.scalar.activation(out=dst, in_=acc, func=ACT.Copy, scale=factor)
 
-        for h, cols in enumerate(HALVES):
-            nc.scalar.activation(out=sg0[:, cols], in_=accs[0, h], func=ACT.Sigmoid)
-            nc.vector.tensor_copy(out=y[0][:, cols], in_=accs[0, h])
-            nc.scalar.copy(out=y[1][:, cols], in_=accs[1, h])
-        gate(1)
-        for t in (2, 3):
+        def empty(engine_copy, t, h):
+            engine_copy(out=y[t][:, HALVES[h]], in_=accs[t, h])
+
+        def late(t):
             nc.scalar.copy(out=y[t][:], in_=accs[t][:])
-            gate(t)
-        for cols in HALVES:
+
+        def plain_gate(h):
+            nc.scalar.activation(out=sg0[:, HALVES[h]], in_=accs[0, h], func=ACT.Sigmoid)
+
+        def gated0(h):
+            cols = HALVES[h]
             nc.vector.tensor_tensor(out=st[0][:, cols], in0=sg0[:].indirect(entries(n1_sb, cols)), in1=y[0][:, cols], op=ALU.mult)
-        w2dw = deal_words("w2dw", ww2)
+
+        plain_gate(0)
+        empty(nc.vector.tensor_copy, 1, 0)
+        empty(nc.vector.tensor_copy, 0, 0)
+        plain_gate(1)
+        empty(nc.vector.tensor_copy, 0, 1)
+        empty(nc.scalar.copy, 1, 1)
+        w2ds = deal_scales("w2ds", ws)
+        gate(1)
+        late(2)
+        gate(2)
+        late(3)
+        gate(3)
+        gated0(0)
+        gated0(1)
         gather_st(0, 0)
         gated(1)
         larger(0, 0)
@@ -179,13 +204,12 @@ def tile_picked_skipcrossbtwicp_none_po_kernel(
         larger(0, 1)
         larger(3, 0)
         weave(nc.scalar.copy, zi[0][:], zp[0][:])
-        w2ds = deal_scales("w2ds", ws)
         gather_st(1, 1)
         gather_st(2, 1)
         larger(1, 1)
+        quantize_z(0)
         gather_st(3, 1)
         larger(2, 1)
-        quantize_z(0)
         larger(3, 1)
         second(0)
 
@@ -198,14 +222,31 @@ def tile_picked_skipcrossbtwicp_none_po_kernel(
         out_rows = out_0.rearrange("(p t) j -> p t j", t=PACK)
         out_words = out_1[0].rearrange("p n t -> p (n t)").bitcast(I32)
 
-        def first_term(t, cols):
-            nc.vector.tensor_tensor(out=p1[:, t, cols], in0=y[t][:].indirect(entries(n3_sb, cols)), in1=hh[t][:, cols], op=ALU.mult)
+        def first_term(t, h):
+            cols = HALVES[h]
+            factor = hp[t, h][:] if (t, h) in SUMMED else hh[t][:, cols]
+            nc.vector.tensor_tensor(out=p1[:, t, cols], in0=y[t][:].indirect(entries(n3_sb, cols)), in1=factor, op=ALU.mult)
 
         def second_term(t, cols):
             nc.vector.tensor_tensor(out=p2[:, t, cols], in0=hw[t][:].indirect(entries(n2_sb, cols)), in1=y[t][:, cols], op=ALU.mult)
 
         def difference(t, cols):
-            nc.vector.tensor_tensor(out=res[:, t, cols], in0=p1[:, t, cols], in1=p2[:, t, cols], op=ALU.subtract)
+            nc.vector.tensor_tensor(out=res[:, t, cols], in0=p2[:, t, cols], in1=p1[:, t, cols], op=ALU.subtract)
+            nc.sync.dma_start(out=out_rows[:, t, cols], in_=res[:, t, cols])
+
+        def total(t, cols):
+            width = cols.stop - cols.start
+            turned = bank(2 * t)
+            for j in range(0, width, P):
+                block = slice(cols.start + j, cols.start + j + P)
+                for term, opens in ((p1, True), (p2, False)):
+                    nc.tensor.matmul(turned[:, j : j + P], lhsT=term[:, t, block], rhs=ident[:], is_transpose=True, start=opens, stop=not opens)
+            turned_sb = tile("turned%d" % t, [P, width], F32)
+            nc.scalar.copy(out=turned_sb[:], in_=turned[:, 0:width])
+            back = bank(2 * t + 1)
+            for j in range(0, width, P):
+                nc.tensor.transpose(back[:, j : j + P], turned_sb[:, j : j + P], ident[:])
+            nc.scalar.copy(out=res[:, t, cols], in_=back[:, 0:width])
             nc.sync.dma_start(out=out_rows[:, t, cols], in_=res[:, t, cols])
 
         def planes(h):
@@ -213,28 +254,34 @@ def tile_picked_skipcrossbtwicp_none_po_kernel(
             nc.vector.quantize_mx(out=ow[:, cols].bitcast(FP8X4), scales=osc[:, cols], in_=ri[h][:].rearrange("p c t -> p (c t)"))
             nc.sync.dma_start(out=out_words[:, cols], in_=ow[:, cols])
 
-        first_term(0, HALVES[0])
+        first_term(0, 0)
         weave(nc.vector.tensor_copy, zi[1][:], zp[1][:])
-        first_term(1, HALVES[0])
+        first_term(1, 0)
         quantize_z(1)
         second(1)
-        first_term(2, HALVES[0])
-        first_term(3, HALVES[0])
-        for t in range(PACK - 1):
-            second_term(t, ALL)
-            first_term(t, HALVES[1])
-            if t > 0:
-                difference(t - 1, ALL)
+        first_term(2, 0)
+        first_term(3, 0)
+        second_term(0, ALL)
+        first_term(0, 1)
+        total(0, ALL)
+        second_term(1, ALL)
+        total(1, HALVES[0])
+        first_term(1, 1)
+        second_term(2, ALL)
+        difference(1, HALVES[1])
+        first_term(2, 1)
         last = PACK - 1
         second_term(last, HALVES[0])
         difference(last - 1, ALL)
         difference(last, HALVES[0])
         weave(nc.scalar.copy, ri[0][:], res[:, :, HALVES[0]])
-        first_term(last, HALVES[1])
-        second_term(last, HALVES[1])
-        difference(last, HALVES[1])
+        first_term(last, 1)
+        for cols in QUARTERS:
+            second_term(last, cols)
+        for cols, engine_copy in zip(QUARTERS, [nc.scalar.copy, nc.vector.tensor_copy]):
+            difference(last, cols)
+            weave(engine_copy, ri[1][:, cols.start - HALF : cols.stop - HALF, :], res[:, :, cols])
         planes(0)
-        weave(nc.vector.tensor_copy, ri[1][:], res[:, :, HALVES[1]])
         planes(1)
         for q in range(4):
             queue = nc.scalar if q % 2 else nc.sync

from contextlib import ExitStack

import concourse.mybir as mybir
from concourse.masks import make_identity

K, T, S, H, N = 512, 2048, 512, 512, 512
FLOPS = 2 * K * H * S + 2 * H * N * S

F32 = mybir.dt.float32
BF16 = mybir.dt.bfloat16
I32 = mybir.dt.int32
U32 = mybir.dt.uint32
U16 = mybir.dt.uint16
U8 = mybir.dt.uint8
FP8X4 = mybir.dt.float8_e4m3fn_x4
FP4X4 = mybir.dt.float4_e2m1fn_x4
ALU = mybir.AluOpType
ACT = mybir.ActivationFunctionType

P = 128
PACK = 4
HALF = S // 2
ALL = slice(0, S)
HALVES = [slice(0, HALF), slice(HALF, S)]
SUMMED = [(0, 0), (0, 1), (1, 0)]
QUARTERS = [slice(256, 384), slice(384, 512)]


def entries(lst, cols):
    return lst[:, cols.start // 16 : cols.stop // 16]


def load_scale_rows(queues, plane, rows):
    for q in range(4):
        queues[q].dma_start(out=plane[32 * q : 32 * q + 4, :].bitcast(I32), in_=rows[4 * q : 4 * q + 4, :].bitcast(I32))


def tile_picked_skipcrossbtwicp_none_po_kernel(
    tc, x_words, x_scales, w1_words, w1_scales, gn, w2_words, w2_scales, offs, n1, n2, n3, out_0, out_1, out_2
):
    nc = tc.nc
    with ExitStack() as ctx:
        sb = ctx.enter_context(tc.tile_pool(name="sb", bufs=1))
        ps = ctx.enter_context(tc.psum_pool(name="ps", bufs=1))

        def tile(name, shape, dtype, tag=None):
            return sb.tile(shape, dtype, name=name, tag=tag or name, align_bytes=64)

        def bank(b):
            return ps.tile([P, 512], F32, name="bank%d" % b)

        offs_sb = tile("offs_sb", [P, S // 16], U16)
        n1_sb = tile("n1_sb", [P, S // 16], U16)
        n2_sb = tile("n2_sb", [P, S // 16], U16)
        n3_sb = tile("n3_sb", [P, S // 16], U16)
        xw = tile("xw", [P, T], I32)
        xs = tile("xs", [P, T], U8)
        ww = tile("ww", [P, 2 * H], U8)
        ws = tile("ws", [P, H], U8)

        nc.gpsimd.memset(xs[:].bitcast(I32), 0)
        nc.gpsimd.memset(ws[:].bitcast(I32), 0)
        nc.sync.dma_start(offs_sb[:], offs)
        nc.sync.dma_start(out=ww[:].bitcast(I32), in_=w1_words[0].bitcast(I32))
        nc.sync.dma_start(n1_sb[:], n1)
        nc.sync.dma_start(n3_sb[:], n3)
        nc.sync.dma_start(n2_sb[:], n2)
        ww2 = tile("ww2", [P, 2 * N], U8)
        nc.sync.dma_start(out=ww2[:].bitcast(I32), in_=w2_words[0].bitcast(I32))
        nc.sync.dma_start(out=xw[:], in_=x_words[0].rearrange("p n t -> p (n t)").bitcast(I32))
        load_scale_rows([nc.scalar] * 4, xs, x_scales[0])
        load_scale_rows([nc.gpsimd] + [nc.scalar] * 3, ws, w1_scales[0])

        def deal_words(name, words):
            dw = tile(name, [P, PACK, P, 2], U8)
            nc.vector.tensor_copy(out=dw[:], in_=words[:].rearrange("p (m t b) -> p t m b", t=PACK, b=2))
            return dw

        def deal_scales(name, scales):
            ds = tile(name, [P, PACK, P], U8)
            nc.vector.tensor_copy(out=ds[:], in_=scales[:].rearrange("p (m t) -> p t m", t=PACK))
            return ds

        def product(acc, dw, ds, t, codes, scales):
            nc.tensor.matmul_mx(
                out=acc,
                lhsT=dw[:, t, :, :].rearrange("p m b -> p (m b)").bitcast(FP4X4),
                lhsT_scale=ds[:, t, :],
                rhs=codes.bitcast(FP8X4),
                rhs_scale=scales,
                start=True,
                stop=True,
            )

        def weave(engine_copy, dst, src):
            engine_copy(
                out=dst.rearrange("p (c i) t -> p c t i", i=2),
                in_=src.rearrange("p t (c i) -> p c t i", i=2),
            )

        w1dw = deal_words("w1dw", ww)
        gain = tile("gain", [P, PACK], F32, tag="ww")
        nc.sync.dma_start(out=gain[:], in_=gn.rearrange("(p t) o -> p (t o)", t=PACK))
        w2dw = deal_words("w2dw", ww2)
        w1ds = deal_scales("w1ds", ws)
        load_scale_rows([nc.sync] * 4, ws, w2_scales[0])
        xgs = [tile("xgs%d" % h, [P, HALF], U8) for h in range(2)]
        xgw = [tile("xgw%d" % h, [P, HALF], U32) for h in range(2)]
        for h, cols in enumerate(HALVES):
            nc.vector.tensor_copy(out=xgs[h][:], in_=xs[:].indirect(entries(offs_sb, cols)))
            nc.vector.tensor_copy(out=xgw[h][:], in_=xw[:].bitcast(U32).indirect(entries(offs_sb, cols)))

        y = [tile("y%d" % t, [P, S], F32) for t in range(PACK)]
        accs = {}
        for t, h in [(0, 0), (1, 0), (0, 1), (1, 1)]:
            accs[t, h] = bank(2 * t + h)[:, 0:HALF]
            product(accs[t, h], w1dw, w1ds, t, xgw[h][:], xgs[h][:])
        for t in (2, 3):
            accs[t] = bank(2 + t)
            for h, cols in enumerate(HALVES):
                product(accs[t][:, cols], w1dw, w1ds, t, xgw[h][:], xgs[h][:])

        sg0 = tile("sg0", [P, S], F32)
        stw = [tile("stw%d" % t, [P, S], F32) for t in range(PACK)]
        sg = [None] + [tile("sg%d" % t, [P, S], F32) for t in range(1, PACK)]
        hw = [tile("hw%d" % t, [P, 2 * S], F32) for t in range(PACK)]
        st = [w[:, 0:S] for w in stw]
        hh = [w[:, 0:S] for w in hw]
        stg = [w[:, S : 2 * S] for w in hw]
        mx = tile("mx", [P, PACK, S], F32)
        hp = {(t, h): tile("hp%d%d" % (t, h), [P, HALF], F32) for t, h in SUMMED}
        ident = tile("ident", [P, P], F32)
        make_identity(nc, ident[:])
        zp = [tile("zp%d" % h, [P, PACK, HALF], BF16) for h in range(2)]
        zi = [tile("zi%d" % h, [P, HALF, PACK], BF16) for h in range(2)]
        zw = [tile("zw%d" % h, [P, HALF], U32) for h in range(2)]
        zs = [tile("zs%d" % h, [P, HALF], U8) for h in range(2)]

        def gather_st(t, h):
            cols = HALVES[h]
            nc.vector.tensor_copy(out=stg[t][:, cols], in_=stw[t][:].indirect(entries(n1_sb, cols)))

        def larger(t, h):
            cols = HALVES[h]
            nc.vector.tensor_tensor(out=mx[:, t, cols], in0=stg[t][:, cols], in1=st[t][:, cols], op=ALU.max)
            nc.scalar.activation(out=zp[h][:, t, :], in_=mx[:, t, cols], func=ACT.Copy, scale=gain[:, t : t + 1])

        def gate(t):
            for cols in HALVES:
                nc.scalar.activation(out=sg[t][:, cols], in_=y[t][:].indirect(entries(n1_sb, cols)), func=ACT.Sigmoid)

        def gated(t):
            nc.vector.tensor_tensor(out=st[t], in0=y[t][:], in1=sg[t][:], op=ALU.mult)

        def quantize_z(h):
            nc.vector.quantize_mx(out=zw[h][:].bitcast(FP8X4), scales=zs[h][:], in_=zi[h][:].rearrange("p c t -> p (c t)"))

        def second(h):
            for t in range(PACK):
                acc = bank(PACK * h + t)[:, 0:HALF]
                product(acc, w2dw, w2ds, t, zw[h][:], zs[h][:])
                copies = [(hh[t][:, HALVES[h]], -0.75)] + ([(hp[t, h][:], 0.75)] if (t, h) in SUMMED else [])
                for dst, factor in copies[::-1] if h == 0 else copies:
                    nc.scalar.activation(out=dst, in_=acc, func=ACT.Copy, scale=factor)

        def empty(engine_copy, t, h):
            engine_copy(out=y[t][:, HALVES[h]], in_=accs[t, h])

        def late(t):
            nc.scalar.copy(out=y[t][:], in_=accs[t][:])

        def plain_gate(h):
            nc.scalar.activation(out=sg0[:, HALVES[h]], in_=accs[0, h], func=ACT.Sigmoid)

        def gated0(h):
            cols = HALVES[h]
            nc.vector.tensor_tensor(out=st[0][:, cols], in0=sg0[:].indirect(entries(n1_sb, cols)), in1=y[0][:, cols], op=ALU.mult)

        plain_gate(0)
        empty(nc.vector.tensor_copy, 1, 0)
        empty(nc.vector.tensor_copy, 0, 0)
        plain_gate(1)
        empty(nc.vector.tensor_copy, 0, 1)
        empty(nc.scalar.copy, 1, 1)
        w2ds = deal_scales("w2ds", ws)
        gate(1)
        late(2)
        gate(2)
        late(3)
        gate(3)
        gated0(0)
        gated0(1)
        gather_st(0, 0)
        gated(1)
        larger(0, 0)
        gather_st(1, 0)
        gather_st(0, 1)
        gated(2)
        larger(1, 0)
        gather_st(2, 0)
        gated(3)
        larger(2, 0)
        gather_st(3, 0)
        larger(0, 1)
        larger(3, 0)
        weave(nc.scalar.copy, zi[0][:], zp[0][:])
        gather_st(1, 1)
        gather_st(2, 1)
        larger(1, 1)
        quantize_z(0)
        gather_st(3, 1)
        larger(2, 1)
        larger(3, 1)
        second(0)

        p1 = tile("p1", [P, PACK, S], F32)
        p2 = tile("p2", [P, PACK, S], F32)
        res = tile("res", [P, PACK, S], F32)
        ri = [tile("ri%d" % h, [P, HALF, PACK], BF16) for h in range(2)]
        ow = tile("ow", [P, S], I32)
        osc = tile("osc", [P, S], U8)
        out_rows = out_0.rearrange("(p t) j -> p t j", t=PACK)
        out_words = out_1[0].rearrange("p n t -> p (n t)").bitcast(I32)

        def first_term(t, h):
            cols = HALVES[h]
            factor = hp[t, h][:] if (t, h) in SUMMED else hh[t][:, cols]
            nc.vector.tensor_tensor(out=p1[:, t, cols], in0=y[t][:].indirect(entries(n3_sb, cols)), in1=factor, op=ALU.mult)

        def second_term(t, cols):
            nc.vector.tensor_tensor(out=p2[:, t, cols], in0=hw[t][:].indirect(entries(n2_sb, cols)), in1=y[t][:, cols], op=ALU.mult)

        def difference(t, cols):
            nc.vector.tensor_tensor(out=res[:, t, cols], in0=p2[:, t, cols], in1=p1[:, t, cols], op=ALU.subtract)
            nc.sync.dma_start(out=out_rows[:, t, cols], in_=res[:, t, cols])

        def total(t, cols):
            width = cols.stop - cols.start
            turned = bank(2 * t)
            for j in range(0, width, P):
                block = slice(cols.start + j, cols.start + j + P)
                for term, opens in ((p1, True), (p2, False)):
                    nc.tensor.matmul(turned[:, j : j + P], lhsT=term[:, t, block], rhs=ident[:], is_transpose=True, start=opens, stop=not opens)
            turned_sb = tile("turned%d" % t, [P, width], F32)
            nc.scalar.copy(out=turned_sb[:], in_=turned[:, 0:width])
            back = bank(2 * t + 1)
            for j in range(0, width, P):
                nc.tensor.transpose(back[:, j : j + P], turned_sb[:, j : j + P], ident[:])
            nc.scalar.copy(out=res[:, t, cols], in_=back[:, 0:width])
            nc.sync.dma_start(out=out_rows[:, t, cols], in_=res[:, t, cols])

        def planes(h):
            cols = HALVES[h]
            nc.vector.quantize_mx(out=ow[:, cols].bitcast(FP8X4), scales=osc[:, cols], in_=ri[h][:].rearrange("p c t -> p (c t)"))
            nc.sync.dma_start(out=out_words[:, cols], in_=ow[:, cols])

        first_term(0, 0)
        weave(nc.vector.tensor_copy, zi[1][:], zp[1][:])
        first_term(1, 0)
        quantize_z(1)
        second(1)
        first_term(2, 0)
        first_term(3, 0)
        second_term(0, ALL)
        first_term(0, 1)
        total(0, ALL)
        second_term(1, ALL)
        total(1, HALVES[0])
        first_term(1, 1)
        second_term(2, ALL)
        difference(1, HALVES[1])
        first_term(2, 1)
        last = PACK - 1
        second_term(last, HALVES[0])
        difference(last - 1, ALL)
        difference(last, HALVES[0])
        weave(nc.scalar.copy, ri[0][:], res[:, :, HALVES[0]])
        first_term(last, 1)
        for cols in QUARTERS:
            second_term(last, cols)
        for cols, engine_copy in zip(QUARTERS, [nc.scalar.copy, nc.vector.tensor_copy]):
            difference(last, cols)
            weave(engine_copy, ri[1][:, cols.start - HALF : cols.stop - HALF, :], res[:, :, cols])
        planes(0)
        planes(1)
        for q in range(4):
            queue = nc.scalar if q % 2 else nc.sync
            queue.dma_start(out=out_2[0][4 * q : 4 * q + 4, :].bitcast(I32), in_=osc[32 * q : 32 * q + 4, :].bitcast(I32))
